import numpy as np, ml_dtypes
CORES = [2,3,42,43,82,83,122,123]
N = 8
import mx_ref
BF = ml_dtypes.bfloat16
def entries(a):
    return np.ascontiguousarray(a.T).reshape(-1)
def table(e):
    return np.ascontiguousarray(np.reshape(e, (-1, 16)).T).astype(np.int32)
def gentries(a):
    return np.ascontiguousarray(a.reshape(8, 16, -1).transpose(0, 2, 1)).reshape(8, -1)
def gtable(e):
    e = np.asarray(e); return np.ascontiguousarray(e.reshape(8, -1, 16).transpose(0, 2, 1)).reshape(128, -1).astype(np.int32)
def cols(t, e):
    v = np.concatenate([t.reshape(128, -1, 4), np.zeros((128, 1, 4), BF)], axis=1)
    return np.ascontiguousarray(v[:, e]).reshape(128, -1)
def gcols(t, e):
    v = np.concatenate([t.reshape(8, 16, -1, 4), np.zeros((8, 16, 1, 4), BF)], axis=2)
    return np.ascontiguousarray(np.stack([v[g][:, e[g]] for g in range(8)])).reshape(128, -1)
def cut(t, i, w=512):
    return t[:, w * i:w * i + w]
def f(rng, *shape):
    return mx_ref.flush((rng.standard_normal(shape, dtype=np.float32) * np.exp2(rng.integers(-2, 3, shape[:-1] + (1,)))).astype(BF))
def wide(rng, *shape, cols=0):
    v = rng.standard_normal(shape, dtype=np.float32) * np.exp2(rng.integers(-12, 13, shape)).astype(np.float32)
    if cols: v *= np.repeat(np.exp2(rng.integers(-cols, cols + 1, shape[:-2] + (1, shape[-1] // 4))) * (rng.random(shape[:-2] + (1, shape[-1] // 4)) > 0.0625), 4, axis=-1).astype(np.float32)
    return mx_ref.flush(v.astype(BF))
T, CAPP, S, O = 256, 64, 512, 2
def lists(rng, kind=""):
    sn = np.full((N, N, CAPP), -1)
    for s in range(N):
        for d in range(N):
            n = CAPP if kind == "foreign" else 0 if kind == "own" else int(rng.integers(0, CAPP + 1))
            if d != s: sn[s, d, rng.permutation(CAPP)[:n]] = rng.integers(0, T, n)
    if kind == "one":
        s, d = rng.permutation(N)[:2]; sn[s, d] = rng.integers(0, T)
    ql = []
    for r in range(N):
        slots = T + np.flatnonzero(sn[:, r].reshape(-1) >= 0)
        if kind == "foreign": e = rng.permutation(np.resize(slots, 4 * S)).reshape(4, S)
        elif kind == "own": e = rng.integers(0, T, (4, S))
        else: e = rng.choice(np.concatenate([np.arange(T), slots]), (4, S))
        if kind == "whole": e = np.repeat(e[:1], 4, axis=0)
        if kind == "one":
            for u in rng.permutation(4)[:int(rng.integers(1, 5))]: e[u] = e[u, 0]
        ql.append(gtable(np.repeat(e, 2, axis=0)))
    return {"sn": np.stack([table(sn[s].reshape(-1)) for s in range(N)]), "ql": np.stack(ql)}
def setup_inputs(rng):
    return {"x": f(rng, N, 128, 4 * T), "w": f(rng, N, 128, O * 512), **lists(rng)}
def setup_inputs_whole(rng):
    return {**setup_inputs(rng), **lists(rng, "whole")}
def setup_inputs_foreign(rng):
    return {**setup_inputs(rng), **lists(rng, "foreign")}
def setup_inputs_own(rng):
    return {**setup_inputs(rng), **lists(rng, "own")}
def setup_inputs_one(rng):
    return {**setup_inputs(rng), **lists(rng, "one")}
def setup_inputs_spread(rng):
    d = setup_inputs(rng); d["x"] = wide(rng, N, 128, 4 * T, cols=8); return d
def check_inputs(d):
    b = []; to = [entries(d["sn"][s]).reshape(N, CAPP) for s in range(N)]
    for r in range(N):
        if to[r].min() < -1 or to[r].max() >= T or (to[r][r] != -1).any(): b.append("sn")
        e = gentries(d["ql"][r]); there = np.concatenate([np.ones(T, bool)] + [to[s][r] >= 0 for s in range(N)])
        if e.min() < 0 or e.max() >= T + N * CAPP or not there[np.clip(e, 0, T + N * CAPP - 1)].all() or (e[0::2] != e[1::2]).any(): b.append("ql")
    return b
def reference(x, w, sn, ql):
    to = [entries(sn[s]).reshape(N, CAPP) for s in range(N)]
    y = np.zeros((N, 128, O * S), np.float32)
    for r in range(N):
        have = np.concatenate([x[r]] + [cols(x[s], to[s][r]) for s in range(N)], axis=1)
        V = mx_ref.quantize(gcols(have, gentries(ql[r])))
        for o in range(O): y[r][:, S * o:S * o + S] = mx_ref.matmul(mx_ref.quantize(np.ascontiguousarray(cut(w[r], o))), V)
    return {"y": y}

@@ -1,0 +1,168 @@
+import numpy as np
+from concourse.bass import DstId, RemoteDMATransfer
+from concourse.mybir import dt, ActivationFunctionType
+
+N, CAPP, TC, S, O = 8, 64, 256, 512, 2
+HV = TC + N * CAPP
+ONCHIP = 2
+COPY = ActivationFunctionType.Copy
+U32, U8 = dt.uint32, dt.uint8
+
+SCRATCH = {
+    "xt": ("sbuf", [128, 4 * TC], "bfloat16"),
+    "wt": ("sbuf", [128, O * 512], "bfloat16"),
+    "snl": ("sbuf", [128, N * CAPP // 16], "int32"),
+    "qll": ("sbuf", [128, S // 16], "int32"),
+    "offs": ("sbuf", [128, N * CAPP // 16], "uint16"),
+    "offq": ("sbuf", [128, S // 16], "uint16"),
+    "xq": ("sbuf", [128, TC], "float8_e4m3fn_x4"),
+    "xs": ("sbuf", [128, TC], "uint8"),
+    "snd": ("sbuf", [128, N * CAPP], "float8_e4m3fn_x4"),
+    "snds": ("sbuf", [128, N * CAPP], "uint8"),
+    "have": ("sbuf", [128, HV], "float8_e4m3fn_x4"),
+    "haves": ("sbuf", [128, HV], "uint8"),
+    "vq": ("sbuf", [128, S], "float8_e4m3fn_x4"),
+    "vs": ("sbuf", [128, S], "uint8"),
+    "wq": ("sbuf", [128, O * 128], "float8_e4m3fn_x4"),
+    "ws": ("sbuf", [128, O * 128], "uint8"),
+    "acc": ("psum", [128, 4 * 512], "float32"),
+    "ysb": ("sbuf", [128, O * S], "float32"),
+}
+SEMAPHORES = (["ldx", "ldsn", "ldql", "ldw", "coff", "qx", "pc0", "pc1", "pz0", "pz1", "qh", "qw", "coq",
+               "arrc", "arrs", "left", "stored"]
+              + ["v%s%d" % (k, h) for k in "cz" for h in range(2)]
+              + ["mm%d" % i for i in range(4)] + ["cp%d" % i for i in range(4)])
+
+
+def plan(T, topo, src):
+    cs = list(T.cores)
+    far, near, own = [], [], []
+    for d in range(N):
+        c = cs[d]
+        if c == src:
+            continue
+        if topo.chip(c) == topo.chip(src):
+            own.append(d)
+        elif topo.same_plane(topo.chip(src), topo.chip(c)):
+            near.append(d)
+        else:
+            far.append(d)
+    waves = []
+    for off, on in ((far, []), (near, own)):
+        wave, free = [], list(topo.engines(src, cs[off[0]]))
+        per = len(free) // len(off)
+        for i, d in enumerate(off):
+            wave.append((d, free[i * per:(i + 1) * per]))
+        for i, d in enumerate(on):
+            more = [e for e in topo.engines(src, cs[d]) if e not in free]
+            wave.append((d, more[i * ONCHIP:(i + 1) * ONCHIP]))
+        waves.append(wave)
+    return waves
+
+
+def rank_program(g, core, T, topo):
+    rank = T.rank_of(core)
+    if rank is None:
+        return
+    sem = T.sem
+    cs = list(T.cores)
+    waves = plan(T, topo, core)
+    V, A, P, Y = g.vector, g.scalar, g.tensor, g.sync
+
+    Y.dma_start(T.xt[:], T.x[:]).then_inc(sem.ldx, 16)
+    for grp in range(8):
+        (Y if grp < 3 else A).dma_start(T.snl[16 * grp:16 * grp + 16, :], T.sn[:]).then_inc(sem.ldsn, 16)
+    Y.wait_ge(sem.ldx, 16)
+    Y.dma_start(T.qll[:], T.ql[:]).then_inc(sem.ldql, 16)
+    Y.dma_start(T.wt[:], T.w[:]).then_inc(sem.ldw, 16)
+
+    runs = []
+    for wave in waves:
+        ds = sorted(d for d, _ in wave)
+        rr = []
+        for d in ds:
+            if rr and rr[-1][1] == d:
+                rr[-1][1] = d + 1
+            else:
+                rr.append([d, d + 1])
+        runs.append(rr)
+
+    V.wait_ge(sem.ldsn, 128)
+    V.tensor_copy(T.offs[:], T.snl[:]).then_inc(sem.coff, 1)
+    V.wait_ge(sem.ldx, 16)
+    V.quantize_mx(T.xq[:, 0:TC], T.xs[:, 0:TC], T.xt[:]).then_inc(sem.qx, 1)
+    V.wait_ge(sem.coff, 1)
+    V.wait_ge(sem.qx, 1)
+    k = CAPP // 16
+    for i, rr in enumerate(runs):
+        for a, b in rr:
+            V.tensor_copy(T.snd[:, CAPP * a:CAPP * b].bitcast(U32),
+                          T.xq[:, 0:TC].bitcast(U32).indirect(T.offs[:, k * a:k * b])).then_inc(sem["pc%d" % i], 1)
+    A.wait_ge(sem.coff, 1)
+    A.wait_ge(sem.qx, 1)
+    for i, rr in enumerate(runs):
+        for a, b in rr:
+            A.activation(T.snds[:, CAPP * a:CAPP * b], T.xs[:, 0:TC].indirect(T.offs[:, k * a:k * b]),
+                         COPY).then_inc(sem["pz%d" % i], 1)
+
+    at = TC + CAPP * rank
+    left = 0
+    for kind in ("c", "z"):
+        for i, wave in enumerate(waves):
+            g.wait_ge(sem["p%s%d" % (kind, i)], len(runs[i]))
+            tr = []
+            for d, eng in wave:
+                rid, pid, _ = topo.addr(cs[d])
+                if kind == "c":
+                    src = T.snd[:, CAPP * d:CAPP * d + CAPP].bitcast(U8)
+                    dst = T.have[:, at:at + CAPP].bitcast(U8)
+                else:
+                    src = T.snds[:, CAPP * d:CAPP * d + CAPP]
+                    dst = T.haves[:, at:at + CAPP]
+                tr.append(RemoteDMATransfer(dst_ids=[DstId(rid=rid, pnc=pid)], dma_engine_mask=sum(1 << e for e in eng),
+                                            remote_sem=sem.arrc if kind == "c" else sem.arrs, src=src, dst=dst))
+                left += len(eng)
+            g.remote_dma_fused(tr, local_sem=sem.left)
+
+    due = 0
+    for s in range(N):
+        if s != rank:
+            due += sum(len(eng) for wave in plan(T, topo, cs[s]) for d, eng in wave if d == rank)
+
+    V.quantize_mx(T.have[:, 0:TC], T.haves[:, 0:TC], T.xt[:]).then_inc(sem.qh, 1)
+    V.wait_ge(sem.ldql, 16)
+    V.tensor_copy(T.offq[:], T.qll[:]).then_inc(sem.coq, 1)
+    V.wait_ge(sem.ldw, 16)
+    V.quantize_mx(T.wq[:, 0:O * 128], T.ws[:, 0:O * 128], T.wt[:]).then_inc(sem.qw, 1)
+
+    H = S // 2
+    V.wait_ge(sem.qh, 1)
+    V.wait_ge(sem.coq, 1)
+    V.wait_ge(sem.arrc, due)
+    A.wait_ge(sem.qh, 1)
+    A.wait_ge(sem.coq, 1)
+    A.wait_ge(sem.arrs, due)
+    for h in range(2):
+        o = T.offq[:, h * H // 16:(h + 1) * H // 16]
+        V.tensor_copy(T.vq[:, h * H:h * H + H].bitcast(U32), T.have[:, 0:HV].bitcast(U32).indirect(o)).then_inc(sem["vc%d" % h], 1)
+        A.activation(T.vs[:, h * H:h * H + H], T.haves[:, 0:HV].indirect(o), COPY).then_inc(sem["vz%d" % h], 1)
+
+    P.wait_ge(sem.qw, 1)
+    for h in range(2):
+        P.wait_ge(sem["vc%d" % h], 1)
+        P.wait_ge(sem["vz%d" % h], 1)
+        for o in range(O):
+            i = 2 * h + o
+            P.matmul_mx(T.acc[:, 512 * i:512 * i + H], T.wq[:, 128 * o:128 * o + 128], T.ws[:, 128 * o:128 * o + 128],
+                        T.vq[:, h * H:h * H + H], T.vs[:, h * H:h * H + H], True, True).then_inc(sem["mm%d" % i], 1)
+            a = S * o + H * h
+            Q = V if o == 0 else A
+            Q.wait_ge(sem["mm%d" % i], 1)
+            if o == 0:
+                V.tensor_copy(T.ysb[:, a:a + H], T.acc[:, 512 * i:512 * i + H]).then_inc(sem["cp%d" % i], 1)
+            else:
+                A.activation(T.ysb[:, a:a + H], T.acc[:, 512 * i:512 * i + H], COPY).then_inc(sem["cp%d" % i], 1)
+            Y.wait_ge(sem["cp%d" % i], 1)
+            Y.dma_start(T.y[:, a:a + H], T.ysb[:, a:a + H]).then_inc(sem.stored, 16)
+    Y.wait_ge(sem.stored, 64)
+    g.wait_ge(sem.left, left)

@@ -4,7 +4,8 @@ from concourse.mybir import dt, ActivationFunctionType
 
 N, CAPP, TC, S, O = 8, 64, 256, 512, 2
 HV = TC + N * CAPP
-ONCHIP = 2
+CHUNKS = [(0, 128), (128, 192), (320, 192)]
+BY_SCALAR = [(1, 1), (2, 1)]
 COPY = ActivationFunctionType.Copy
 U32, U8 = dt.uint32, dt.uint8
 
@@ -25,39 +26,48 @@ SCRATCH = {
     "vs": ("sbuf", [128, S], "uint8"),
     "wq": ("sbuf", [128, O * 128], "float8_e4m3fn_x4"),
     "ws": ("sbuf", [128, O * 128], "uint8"),
-    "acc": ("psum", [128, 4 * 512], "float32"),
+    "acc": ("psum", [128, 6 * 512], "float32"),
     "ysb": ("sbuf", [128, O * S], "float32"),
 }
-SEMAPHORES = (["ldx", "ldsn", "ldql", "ldw", "coff", "qx", "pc0", "pc1", "pz0", "pz1", "qh", "qw", "coq",
-               "arrc", "arrs", "left", "stored"]
-              + ["v%s%d" % (k, h) for k in "cz" for h in range(2)]
-              + ["mm%d" % i for i in range(4)] + ["cp%d" % i for i in range(4)])
+SEMAPHORES = (["ldx", "ldsn", "ldql", "ldw", "coff", "qx", "qh", "qw", "coq", "arrc", "arrz", "left", "stored"]
+              + ["p%s%d" % (k, i) for k in "cz" for i in range(4)]
+              + ["v%s%d" % (k, h) for k in "cz" for h in range(3)]
+              + ["mm%d" % i for i in range(6)] + ["cp%d" % i for i in range(6)])
 
 
 def plan(T, topo, src):
     cs = list(T.cores)
+    me = cs.index(src)
     far, near, own = [], [], []
-    for d in range(N):
-        c = cs[d]
-        if c == src:
-            continue
-        if topo.chip(c) == topo.chip(src):
+    for i in range(1, N):
+        d = (me + i) % N
+        if topo.chip(cs[d]) == topo.chip(src):
             own.append(d)
-        elif topo.same_plane(topo.chip(src), topo.chip(c)):
-            near.append(d)
         else:
-            far.append(d)
-    waves = []
-    for off, on in ((far, []), (near, own)):
-        wave, free = [], list(topo.engines(src, cs[off[0]]))
-        per = len(free) // len(off)
-        for i, d in enumerate(off):
-            wave.append((d, free[i * per:(i + 1) * per]))
-        for i, d in enumerate(on):
-            more = [e for e in topo.engines(src, cs[d]) if e not in free]
-            wave.append((d, more[i * ONCHIP:(i + 1) * ONCHIP]))
-        waves.append(wave)
-    return waves
+            (near if topo.same_plane(topo.chip(src), topo.chip(cs[d])) else far).append(d)
+    near.sort()
+    od = own[0]
+    fc = []
+    for d in far:
+        m = [q for q in fc if topo.chip(cs[q[0]]) == topo.chip(cs[d])]
+        (m[0].append(d) if m else fc.append([d]))
+    fc = [sorted(q) for q in fc]
+    picks = [fc[0], fc[1], near, [od]]
+    e = list(topo.engines(src, cs[far[0]]))
+    m = [k for k in topo.engines(src, cs[od]) if k not in e][0::2]
+    pair = lambda q, per: [(d, e[i * per:(i + 1) * per]) for i, d in enumerate(q)]
+    here = [(od, m)]
+    out = [("c", 0, pair(fc[0], 4)), ("c", 1, pair(fc[1], 4)), ("c", 2, pair(near, 4)),
+           ("z", 1, pair(fc[0] + fc[1], 2)), ("c", 3, here), ("z", 3, pair(near, 4) + here)]
+    return picks, out
+
+
+def transfer(T, topo, kind, to, eng, sem, src, dst):
+    rid, pid, _ = topo.addr(to)
+    if kind == "c":
+        src, dst = src.bitcast(U8), dst.bitcast(U8)
+    return RemoteDMATransfer(dst_ids=[DstId(rid=rid, pnc=pid)], dma_engine_mask=sum(1 << k for k in eng), remote_sem=sem,
+                             src=src, dst=dst)
 
 
 def rank_program(g, core, T, topo):
@@ -66,68 +76,50 @@ def rank_program(g, core, T, topo):
         return
     sem = T.sem
     cs = list(T.cores)
-    waves = plan(T, topo, core)
+    picks, out = plan(T, topo, core)
     V, A, P, Y = g.vector, g.scalar, g.tensor, g.sync
 
     Y.dma_start(T.xt[:], T.x[:]).then_inc(sem.ldx, 16)
     for grp in range(8):
         (Y if grp < 3 else A).dma_start(T.snl[16 * grp:16 * grp + 16, :], T.sn[:]).then_inc(sem.ldsn, 16)
-    Y.wait_ge(sem.ldx, 16)
-    Y.dma_start(T.qll[:], T.ql[:]).then_inc(sem.ldql, 16)
-    Y.dma_start(T.wt[:], T.w[:]).then_inc(sem.ldw, 16)
+    A.dma_start(T.wt[:], T.w[:]).then_inc(sem.ldw, 16)
+    A.dma_start(T.qll[:], T.ql[:]).then_inc(sem.ldql, 16)
 
-    runs = []
-    for wave in waves:
-        ds = sorted(d for d, _ in wave)
-        rr = []
-        for d in ds:
-            if rr and rr[-1][1] == d:
-                rr[-1][1] = d + 1
-            else:
-                rr.append([d, d + 1])
-        runs.append(rr)
-
-    V.wait_ge(sem.ldsn, 128)
-    V.tensor_copy(T.offs[:], T.snl[:]).then_inc(sem.coff, 1)
     V.wait_ge(sem.ldx, 16)
     V.quantize_mx(T.xq[:, 0:TC], T.xs[:, 0:TC], T.xt[:]).then_inc(sem.qx, 1)
-    V.wait_ge(sem.coff, 1)
-    V.wait_ge(sem.qx, 1)
+    V.wait_ge(sem.ldsn, 128)
+    V.tensor_copy(T.offs[:], T.snl[:]).then_inc(sem.coff, 1)
     k = CAPP // 16
-    for i, rr in enumerate(runs):
-        for a, b in rr:
-            V.tensor_copy(T.snd[:, CAPP * a:CAPP * b].bitcast(U32),
-                          T.xq[:, 0:TC].bitcast(U32).indirect(T.offs[:, k * a:k * b])).then_inc(sem["pc%d" % i], 1)
-    A.wait_ge(sem.coff, 1)
-    A.wait_ge(sem.qx, 1)
-    for i, rr in enumerate(runs):
-        for a, b in rr:
-            A.activation(T.snds[:, CAPP * a:CAPP * b], T.xs[:, 0:TC].indirect(T.offs[:, k * a:k * b]),
-                         COPY).then_inc(sem["pz%d" % i], 1)
+    for Q in (V, A):
+        Q.wait_ge(sem.qx, 1)
+        Q.wait_ge(sem.coff, 1)
+    for i, q in enumerate(picks):
+        a, b = q[0], q[-1] + 1
+        o = T.offs[:, k * a:k * b]
+        V.tensor_copy(T.snd[:, CAPP * a:CAPP * b].bitcast(U32),
+                      T.xq[:, 0:TC].bitcast(U32).indirect(o)).then_inc(sem["pc%d" % i], 1)
+        A.activation(T.snds[:, CAPP * a:CAPP * b], T.xs[:, 0:TC].indirect(o), COPY).then_inc(sem["pz%d" % i], 1)
 
     at = TC + CAPP * rank
     left = 0
-    for kind in ("c", "z"):
-        for i, wave in enumerate(waves):
-            g.wait_ge(sem["p%s%d" % (kind, i)], len(runs[i]))
-            tr = []
-            for d, eng in wave:
-                rid, pid, _ = topo.addr(cs[d])
-                if kind == "c":
-                    src = T.snd[:, CAPP * d:CAPP * d + CAPP].bitcast(U8)
-                    dst = T.have[:, at:at + CAPP].bitcast(U8)
-                else:
-                    src = T.snds[:, CAPP * d:CAPP * d + CAPP]
-                    dst = T.haves[:, at:at + CAPP]
-                tr.append(RemoteDMATransfer(dst_ids=[DstId(rid=rid, pnc=pid)], dma_engine_mask=sum(1 << e for e in eng),
-                                            remote_sem=sem.arrc if kind == "c" else sem.arrs, src=src, dst=dst))
-                left += len(eng)
-            g.remote_dma_fused(tr, local_sem=sem.left)
+    seen = {"c": 0, "z": 0}
+    for kind, last, wave in out:
+        while seen[kind] <= last:
+            g.wait_ge(sem["p%s%d" % (kind, seen[kind])], 1)
+            seen[kind] += 1
+        tr = []
+        for d, eng in wave:
+            src = (T.snd if kind == "c" else T.snds)[:, CAPP * d:CAPP * d + CAPP]
+            dst = (T.have if kind == "c" else T.haves)[:, at:at + CAPP]
+            tr.append(transfer(T, topo, kind, cs[d], eng, sem["arr" + kind], src, dst))
+            left += len(eng)
+        g.remote_dma_fused(tr, local_sem=sem.left)
 
-    due = 0
-    for s in range(N):
-        if s != rank:
-            due += sum(len(eng) for wave in plan(T, topo, cs[s]) for d, eng in wave if d == rank)
+    due = {"c": 0, "z": 0}
+    for c in cs:
+        if c != core:
+            for kind in "cz":
+                due[kind] += sum(len(q) for kk, _, wave in plan(T, topo, c)[1] if kk == kind for d, q in wave if d == rank)
 
     V.quantize_mx(T.have[:, 0:TC], T.haves[:, 0:TC], T.xt[:]).then_inc(sem.qh, 1)
     V.wait_ge(sem.ldql, 16)
@@ -135,34 +127,32 @@ def rank_program(g, core, T, topo):
     V.wait_ge(sem.ldw, 16)
     V.quantize_mx(T.wq[:, 0:O * 128], T.ws[:, 0:O * 128], T.wt[:]).then_inc(sem.qw, 1)
 
-    H = S // 2
-    V.wait_ge(sem.qh, 1)
-    V.wait_ge(sem.coq, 1)
-    V.wait_ge(sem.arrc, due)
-    A.wait_ge(sem.qh, 1)
-    A.wait_ge(sem.coq, 1)
-    A.wait_ge(sem.arrs, due)
-    for h in range(2):
-        o = T.offq[:, h * H // 16:(h + 1) * H // 16]
-        V.tensor_copy(T.vq[:, h * H:h * H + H].bitcast(U32), T.have[:, 0:HV].bitcast(U32).indirect(o)).then_inc(sem["vc%d" % h], 1)
-        A.activation(T.vs[:, h * H:h * H + H], T.haves[:, 0:HV].indirect(o), COPY).then_inc(sem["vz%d" % h], 1)
+    for Q, s in ((V, "c"), (A, "z")):
+        Q.wait_ge(sem.qh, 1)
+        Q.wait_ge(sem.coq, 1)
+        Q.wait_ge(sem["arr" + s], due[s])
+    for h, (a, n) in enumerate(CHUNKS):
+        off = T.offq[:, a // 16:(a + n) // 16]
+        V.tensor_copy(T.vq[:, a:a + n].bitcast(U32), T.have[:, 0:HV].bitcast(U32).indirect(off)).then_inc(sem["vc%d" % h], 1)
+        A.activation(T.vs[:, a:a + n], T.haves[:, 0:HV].indirect(off), COPY).then_inc(sem["vz%d" % h], 1)
 
     P.wait_ge(sem.qw, 1)
-    for h in range(2):
+    for h, (b, n) in enumerate(CHUNKS):
         P.wait_ge(sem["vc%d" % h], 1)
         P.wait_ge(sem["vz%d" % h], 1)
         for o in range(O):
             i = 2 * h + o
-            P.matmul_mx(T.acc[:, 512 * i:512 * i + H], T.wq[:, 128 * o:128 * o + 128], T.ws[:, 128 * o:128 * o + 128],
-                        T.vq[:, h * H:h * H + H], T.vs[:, h * H:h * H + H], True, True).then_inc(sem["mm%d" % i], 1)
-            a = S * o + H * h
-            Q = V if o == 0 else A
-            Q.wait_ge(sem["mm%d" % i], 1)
-            if o == 0:
-                V.tensor_copy(T.ysb[:, a:a + H], T.acc[:, 512 * i:512 * i + H]).then_inc(sem["cp%d" % i], 1)
+            acc = T.acc[:, 512 * i:512 * i + n]
+            P.matmul_mx(acc, T.wq[:, 128 * o:128 * o + 128], T.ws[:, 128 * o:128 * o + 128],
+                        T.vq[:, b:b + n], T.vs[:, b:b + n], True, True).then_inc(sem["mm%d" % i], 1)
+            a = S * o + b
+            if (h, o) in BY_SCALAR:
+                A.wait_ge(sem["mm%d" % i], 1)
+                A.activation(T.ysb[:, a:a + n], acc, COPY).then_inc(sem["cp%d" % i], 1)
             else:
-                A.activation(T.ysb[:, a:a + H], T.acc[:, 512 * i:512 * i + H], COPY).then_inc(sem["cp%d" % i], 1)
+                V.wait_ge(sem["mm%d" % i], 1)
+                V.tensor_copy(T.ysb[:, a:a + n], acc).then_inc(sem["cp%d" % i], 1)
             Y.wait_ge(sem["cp%d" % i], 1)
-            Y.dma_start(T.y[:, a:a + H], T.ysb[:, a:a + H]).then_inc(sem.stored, 16)
-    Y.wait_ge(sem.stored, 64)
+            Y.dma_start(T.y[:, a:a + n], T.ysb[:, a:a + n]).then_inc(sem.stored, 16)
+    Y.wait_ge(sem.stored, 6 * 16)
     g.wait_ge(sem.left, left)

@@ -5,7 +5,7 @@ from concourse.mybir import dt, ActivationFunctionType
 N, CAPP, TC, S, O = 8, 64, 256, 512, 2
 HV = TC + N * CAPP
 CHUNKS = [(0, 128), (128, 192), (320, 192)]
-BY_SCALAR = [(1, 1), (2, 1)]
+BY_SCALAR = [(2, 1)]
 COPY = ActivationFunctionType.Copy
 U32, U8 = dt.uint32, dt.uint8
 
@@ -20,6 +20,8 @@ SCRATCH = {
     "xs": ("sbuf", [128, TC], "uint8"),
     "snd": ("sbuf", [128, N * CAPP], "float8_e4m3fn_x4"),
     "snds": ("sbuf", [128, N * CAPP], "uint8"),
+    "hand": ("sbuf", [128, CAPP], "float8_e4m3fn_x4"),
+    "hands": ("sbuf", [128, 2 * CAPP], "uint8"),
     "have": ("sbuf", [128, HV], "float8_e4m3fn_x4"),
     "haves": ("sbuf", [128, HV], "uint8"),
     "vq": ("sbuf", [128, S], "float8_e4m3fn_x4"),
@@ -29,97 +31,141 @@ SCRATCH = {
     "acc": ("psum", [128, 6 * 512], "float32"),
     "ysb": ("sbuf", [128, O * S], "float32"),
 }
-SEMAPHORES = (["ldx", "ldsn", "ldql", "ldw", "coff", "qx", "qh", "qw", "coq", "arrc", "arrz", "left", "stored"]
-              + ["p%s%d" % (k, i) for k in "cz" for i in range(4)]
+SEMAPHORES = (["ldx0", "ldx1", "ldsn", "ldql", "ldw", "coff", "qx", "qh", "qw", "coq", "arrc", "arrz", "hanc", "hanz", "left",
+               "stored"]
+              + ["p%s%d" % (k, i) for k in "cz" for i in range(5)]
               + ["v%s%d" % (k, h) for k in "cz" for h in range(3)]
               + ["mm%d" % i for i in range(6)] + ["cp%d" % i for i in range(6)])
 
 
-def plan(T, topo, src):
+def peers(T, topo, src):
     cs = list(T.cores)
     me = cs.index(src)
-    far, near, own = [], [], []
+    k = [c for c in cs if topo.chip(c) == topo.chip(src)].index(src)
+    fc, near, own = [], [], []
     for i in range(1, N):
         d = (me + i) % N
         if topo.chip(cs[d]) == topo.chip(src):
             own.append(d)
+        elif topo.same_plane(topo.chip(src), topo.chip(cs[d])):
+            near.append(d)
         else:
-            (near if topo.same_plane(topo.chip(src), topo.chip(cs[d])) else far).append(d)
-    near.sort()
-    od = own[0]
-    fc = []
-    for d in far:
-        m = [q for q in fc if topo.chip(cs[q[0]]) == topo.chip(cs[d])]
-        (m[0].append(d) if m else fc.append([d]))
+            m = [q for q in fc if topo.chip(cs[q[0]]) == topo.chip(cs[d])]
+            (m[0].append(d) if m else fc.append([d]))
     fc = [sorted(q) for q in fc]
-    picks = [fc[0], fc[1], near, [od]]
-    e = list(topo.engines(src, cs[far[0]]))
-    m = [k for k in topo.engines(src, cs[od]) if k not in e][0::2]
-    pair = lambda q, per: [(d, e[i * per:(i + 1) * per]) for i, d in enumerate(q)]
-    here = [(od, m)]
-    out = [("c", 0, pair(fc[0], 4)), ("c", 1, pair(fc[1], 4)), ("c", 2, pair(near, 4)),
-           ("z", 1, pair(fc[0] + fc[1], 2)), ("c", 3, here), ("z", 3, pair(near, 4) + here)]
-    return picks, out
+    near.sort()
+    near = near[k:] + near[:k]
+    free = [c for c in topo.cores_of(src)
+            if c not in cs and topo.die(c) != topo.die(src) and topo.may_write(c, cs[near[0]])]
+    return fc, near, own[0], free[k]
 
 
-def transfer(T, topo, kind, to, eng, sem, src, dst):
-    rid, pid, _ = topo.addr(to)
-    if kind == "c":
-        src, dst = src.bitcast(U8), dst.bitcast(U8)
-    return RemoteDMATransfer(dst_ids=[DstId(rid=rid, pnc=pid)], dma_engine_mask=sum(1 << k for k in eng), remote_sem=sem,
-                             src=src, dst=dst)
+def handed_by(T, topo, core):
+    for c in T.cores:
+        if topo.chip(c) == topo.chip(core) and peers(T, topo, c)[3] == core:
+            return c
+    return None
+
+
+def plan(T, topo, core):
+    cs = list(T.cores)
+    if core in cs:
+        fc, near, od, hand = peers(T, topo, core)
+        at = TC + CAPP * cs.index(core)
+        e = list(topo.engines(core, cs[fc[0][0]]))
+        m = [k for k in topo.engines(core, cs[od]) if k not in e]
+        half, per = len(e) // 2, len(e) // 4
+
+        def c(d, eng):
+            return (cs[d], "c", ("snd", CAPP * d, CAPP), ("have", at, CAPP), eng, "arrc")
+
+        def z(d, eng):
+            return (cs[d], "z", ("snds", CAPP * d, CAPP), ("haves", at, CAPP), eng, "arrz")
+
+        return [([("pc", 0)], [(hand, "c", ("snd", CAPP * near[0], CAPP), ("hand", 0, CAPP), m, "hanc")]),
+                ([("pc", 1)], [c(fc[0][0], e[:half]), c(fc[0][1], e[half:])]),
+                ([("pz", 0), ("pz", 3)],
+                 [(hand, "z", ("snds", CAPP * min(near), 2 * CAPP), ("hands", 0, 2 * CAPP), m, "hanz")]),
+                ([("pc", 2), ("pc", 4)], [c(fc[1][0], e[:half]), c(fc[1][1], e[half:]), c(od, m[0::2])]),
+                ([("pc", 3)], [c(near[1], e)]),
+                ([("pz", 1), ("pz", 2), ("pz", 4)],
+                 [z(d, e[per * i:per * i + per]) for i, d in enumerate(fc[0] + fc[1])] + [z(od, m[0::2])])]
+    src = handed_by(T, topo, core)
+    near = peers(T, topo, src)[1]
+    at = TC + CAPP * cs.index(src)
+    e = list(topo.engines(core, cs[near[0]]))
+    half = len(e) // 2
+    return [("hanc", [(cs[near[0]], "c", ("hand", 0, CAPP), ("have", at, CAPP), e, "arrc")]),
+            ("hanz", [(cs[d], "z", ("hands", CAPP * i, CAPP), ("haves", at, CAPP), e[half * i:half * i + half], "arrz")
+                      for i, d in enumerate(sorted(near))])]
+
+
+def call(g, T, topo, wave):
+    tr = []
+    for to, kind, (sb, sc, n), (db, dc, _), eng, sem in wave:
+        src, dst = T[sb][:, sc:sc + n], T[db][:, dc:dc + n]
+        if kind == "c":
+            src, dst = src.bitcast(U8), dst.bitcast(U8)
+        rid, pid, _ = topo.addr(to)
+        tr.append(RemoteDMATransfer(dst_ids=[DstId(rid=rid, pnc=pid)], dma_engine_mask=sum(1 << k for k in eng),
+                                    remote_sem=T.sem[sem], src=src, dst=dst))
+    g.remote_dma_fused(tr, local_sem=T.sem.left)
+    return sum(len(t[4]) for t in wave)
+
+
+def due(T, topo, core, senders, sem):
+    return sum(len(t[4]) for s in senders for _, wave in plan(T, topo, s) for t in wave if t[0] == core and t[5] == sem)
 
 
 def rank_program(g, core, T, topo):
-    rank = T.rank_of(core)
-    if rank is None:
-        return
     sem = T.sem
     cs = list(T.cores)
-    picks, out = plan(T, topo, core)
+    if T.rank_of(core) is None:
+        mine = handed_by(T, topo, core)
+        if mine is None:
+            return
+        left = 0
+        for s, wave in plan(T, topo, core):
+            g.wait_ge(sem[s], due(T, topo, core, [mine], s))
+            left += call(g, T, topo, wave)
+        g.wait_ge(sem.left, left)
+        return
+    fc, near, od, _ = peers(T, topo, core)
     V, A, P, Y = g.vector, g.scalar, g.tensor, g.sync
 
-    Y.dma_start(T.xt[:], T.x[:]).then_inc(sem.ldx, 16)
+    half = 2 * TC
+    for i in range(2):
+        Y.dma_start(T.xt[:, half * i:half * i + half], T.x[:, half * i:half * i + half]).then_inc(sem["ldx%d" % i], 16)
     for grp in range(8):
         (Y if grp < 3 else A).dma_start(T.snl[16 * grp:16 * grp + 16, :], T.sn[:]).then_inc(sem.ldsn, 16)
     A.dma_start(T.wt[:], T.w[:]).then_inc(sem.ldw, 16)
     A.dma_start(T.qll[:], T.ql[:]).then_inc(sem.ldql, 16)
 
-    V.wait_ge(sem.ldx, 16)
-    V.quantize_mx(T.xq[:, 0:TC], T.xs[:, 0:TC], T.xt[:]).then_inc(sem.qx, 1)
+    for i in range(2):
+        V.wait_ge(sem["ldx%d" % i], 16)
+        a, b = TC // 2 * i, TC // 2 * i + TC // 2
+        V.quantize_mx(T.xq[:, a:b], T.xs[:, a:b], T.xt[:, 4 * a:4 * b]).then_inc(sem.qx, 1)
     V.wait_ge(sem.ldsn, 128)
     V.tensor_copy(T.offs[:], T.snl[:]).then_inc(sem.coff, 1)
     k = CAPP // 16
     for Q in (V, A):
-        Q.wait_ge(sem.qx, 1)
+        Q.wait_ge(sem.qx, 2)
         Q.wait_ge(sem.coff, 1)
-    for i, q in enumerate(picks):
-        a, b = q[0], q[-1] + 1
-        o = T.offs[:, k * a:k * b]
+    picks = [[near[0]], fc[0], fc[1], [near[1]], [od]]
+    for i in (0, 1, 2, 3, 4):
+        a, b = picks[i][0], picks[i][-1] + 1
         V.tensor_copy(T.snd[:, CAPP * a:CAPP * b].bitcast(U32),
-                      T.xq[:, 0:TC].bitcast(U32).indirect(o)).then_inc(sem["pc%d" % i], 1)
-        A.activation(T.snds[:, CAPP * a:CAPP * b], T.xs[:, 0:TC].indirect(o), COPY).then_inc(sem["pz%d" % i], 1)
+                      T.xq[:, 0:TC].bitcast(U32).indirect(T.offs[:, k * a:k * b])).then_inc(sem["pc%d" % i], 1)
+    for i in (0, 3, 1, 2, 4):
+        a, b = picks[i][0], picks[i][-1] + 1
+        A.activation(T.snds[:, CAPP * a:CAPP * b],
+                     T.xs[:, 0:TC].indirect(T.offs[:, k * a:k * b]), COPY).then_inc(sem["pz%d" % i], 1)
 
-    at = TC + CAPP * rank
     left = 0
-    seen = {"c": 0, "z": 0}
-    for kind, last, wave in out:
-        while seen[kind] <= last:
-            g.wait_ge(sem["p%s%d" % (kind, seen[kind])], 1)
-            seen[kind] += 1
-        tr = []
-        for d, eng in wave:
-            src = (T.snd if kind == "c" else T.snds)[:, CAPP * d:CAPP * d + CAPP]
-            dst = (T.have if kind == "c" else T.haves)[:, at:at + CAPP]
-            tr.append(transfer(T, topo, kind, cs[d], eng, sem["arr" + kind], src, dst))
-            left += len(eng)
-        g.remote_dma_fused(tr, local_sem=sem.left)
-
-    due = {"c": 0, "z": 0}
-    for c in cs:
-        if c != core:
-            for kind in "cz":
-                due[kind] += sum(len(q) for kk, _, wave in plan(T, topo, c)[1] if kk == kind for d, q in wave if d == rank)
+    for need, wave in plan(T, topo, core):
+        for s, i in need:
+            g.wait_ge(sem["%s%d" % (s, i)], 1)
+        left += call(g, T, topo, wave)
 
     V.quantize_mx(T.have[:, 0:TC], T.haves[:, 0:TC], T.xt[:]).then_inc(sem.qh, 1)
     V.wait_ge(sem.ldql, 16)
@@ -127,10 +173,12 @@ def rank_program(g, core, T, topo):
     V.wait_ge(sem.ldw, 16)
     V.quantize_mx(T.wq[:, 0:O * 128], T.ws[:, 0:O * 128], T.wt[:]).then_inc(sem.qw, 1)
 
-    for Q, s in ((V, "c"), (A, "z")):
+    senders = [c for c in cs if c != core]
+    senders += [peers(T, topo, c)[3] for c in senders]
+    for Q, s in ((V, "arrc"), (A, "arrz")):
         Q.wait_ge(sem.qh, 1)
         Q.wait_ge(sem.coq, 1)
-        Q.wait_ge(sem["arr" + s], due[s])
+        Q.wait_ge(sem[s], due(T, topo, core, senders, s))
     for h, (a, n) in enumerate(CHUNKS):
         off = T.offq[:, a // 16:(a + n) // 16]
         V.tensor_copy(T.vq[:, a:a + n].bitcast(U32), T.have[:, 0:HV].bitcast(U32).indirect(off)).then_inc(sem["vc%d" % h], 1)

import numpy as np
from concourse.bass import DstId, RemoteDMATransfer
from concourse.mybir import dt, ActivationFunctionType

N, CAPP, TC, S, O = 8, 64, 256, 512, 2
HV = TC + N * CAPP
CHUNKS = [(0, 128), (128, 192), (320, 192)]
BY_SCALAR = [(2, 1)]
COPY = ActivationFunctionType.Copy
U32, U8 = dt.uint32, dt.uint8

SCRATCH = {
    "xt": ("sbuf", [128, 4 * TC], "bfloat16"),
    "wt": ("sbuf", [128, O * 512], "bfloat16"),
    "snl": ("sbuf", [128, N * CAPP // 16], "int32"),
    "qll": ("sbuf", [128, S // 16], "int32"),
    "offs": ("sbuf", [128, N * CAPP // 16], "uint16"),
    "offq": ("sbuf", [128, S // 16], "uint16"),
    "xq": ("sbuf", [128, TC], "float8_e4m3fn_x4"),
    "xs": ("sbuf", [128, TC], "uint8"),
    "snd": ("sbuf", [128, N * CAPP], "float8_e4m3fn_x4"),
    "snds": ("sbuf", [128, N * CAPP], "uint8"),
    "hand": ("sbuf", [128, CAPP], "float8_e4m3fn_x4"),
    "hands": ("sbuf", [128, 2 * CAPP], "uint8"),
    "have": ("sbuf", [128, HV], "float8_e4m3fn_x4"),
    "haves": ("sbuf", [128, HV], "uint8"),
    "vq": ("sbuf", [128, S], "float8_e4m3fn_x4"),
    "vs": ("sbuf", [128, S], "uint8"),
    "wq": ("sbuf", [128, O * 128], "float8_e4m3fn_x4"),
    "ws": ("sbuf", [128, O * 128], "uint8"),
    "acc": ("psum", [128, 6 * 512], "float32"),
    "ysb": ("sbuf", [128, O * S], "float32"),
}
SEMAPHORES = (["ldx0", "ldx1", "ldsn", "ldql", "ldw", "coff", "qx", "qh", "qw", "coq", "arrc", "arrz", "hanc", "hanz", "left",
               "stored"]
              + ["p%s%d" % (k, i) for k in "cz" for i in range(5)]
              + ["v%s%d" % (k, h) for k in "cz" for h in range(3)]
              + ["mm%d" % i for i in range(6)] + ["cp%d" % i for i in range(6)])


def peers(T, topo, src):
    cs = list(T.cores)
    me = cs.index(src)
    k = [c for c in cs if topo.chip(c) == topo.chip(src)].index(src)
    fc, near, own = [], [], []
    for i in range(1, N):
        d = (me + i) % N
        if topo.chip(cs[d]) == topo.chip(src):
            own.append(d)
        elif topo.same_plane(topo.chip(src), topo.chip(cs[d])):
            near.append(d)
        else:
            m = [q for q in fc if topo.chip(cs[q[0]]) == topo.chip(cs[d])]
            (m[0].append(d) if m else fc.append([d]))
    fc = [sorted(q) for q in fc]
    near.sort()
    near = near[k:] + near[:k]
    free = [c for c in topo.cores_of(src)
            if c not in cs and topo.die(c) != topo.die(src) and topo.may_write(c, cs[near[0]])]
    return fc, near, own[0], free[k]


def handed_by(T, topo, core):
    for c in T.cores:
        if topo.chip(c) == topo.chip(core) and peers(T, topo, c)[3] == core:
            return c
    return None


def plan(T, topo, core):
    cs = list(T.cores)
    if core in cs:
        fc, near, od, hand = peers(T, topo, core)
        at = TC + CAPP * cs.index(core)
        e = list(topo.engines(core, cs[fc[0][0]]))
        m = [k for k in topo.engines(core, cs[od]) if k not in e]
        half, per = len(e) // 2, len(e) // 4

        def c(d, eng):
            return (cs[d], "c", ("snd", CAPP * d, CAPP), ("have", at, CAPP), eng, "arrc")

        def z(d, eng):
            return (cs[d], "z", ("snds", CAPP * d, CAPP), ("haves", at, CAPP), eng, "arrz")

        return [([("pc", 0)], [(hand, "c", ("snd", CAPP * near[0], CAPP), ("hand", 0, CAPP), m, "hanc")]),
                ([("pc", 1)], [c(fc[0][0], e[:half]), c(fc[0][1], e[half:])]),
                ([("pz", 0), ("pz", 3)],
                 [(hand, "z", ("snds", CAPP * min(near), 2 * CAPP), ("hands", 0, 2 * CAPP), m, "hanz")]),
                ([("pc", 2), ("pc", 4)], [c(fc[1][0], e[:half]), c(fc[1][1], e[half:]), c(od, m[0::2])]),
                ([("pc", 3)], [c(near[1], e)]),
                ([("pz", 1), ("pz", 2), ("pz", 4)],
                 [z(d, e[per * i:per * i + per]) for i, d in enumerate(fc[0] + fc[1])] + [z(od, m[0::2])])]
    src = handed_by(T, topo, core)
    near = peers(T, topo, src)[1]
    at = TC + CAPP * cs.index(src)
    e = list(topo.engines(core, cs[near[0]]))
    half = len(e) // 2
    return [("hanc", [(cs[near[0]], "c", ("hand", 0, CAPP), ("have", at, CAPP), e, "arrc")]),
            ("hanz", [(cs[d], "z", ("hands", CAPP * i, CAPP), ("haves", at, CAPP), e[half * i:half * i + half], "arrz")
                      for i, d in enumerate(sorted(near))])]


def call(g, T, topo, wave):
    tr = []
    for to, kind, (sb, sc, n), (db, dc, _), eng, sem in wave:
        src, dst = T[sb][:, sc:sc + n], T[db][:, dc:dc + n]
        if kind == "c":
            src, dst = src.bitcast(U8), dst.bitcast(U8)
        rid, pid, _ = topo.addr(to)
        tr.append(RemoteDMATransfer(dst_ids=[DstId(rid=rid, pnc=pid)], dma_engine_mask=sum(1 << k for k in eng),
                                    remote_sem=T.sem[sem], src=src, dst=dst))
    g.remote_dma_fused(tr, local_sem=T.sem.left)
    return sum(len(t[4]) for t in wave)


def due(T, topo, core, senders, sem):
    return sum(len(t[4]) for s in senders for _, wave in plan(T, topo, s) for t in wave if t[0] == core and t[5] == sem)


def rank_program(g, core, T, topo):
    sem = T.sem
    cs = list(T.cores)
    if T.rank_of(core) is None:
        mine = handed_by(T, topo, core)
        if mine is None:
            return
        left = 0
        for s, wave in plan(T, topo, core):
            g.wait_ge(sem[s], due(T, topo, core, [mine], s))
            left += call(g, T, topo, wave)
        g.wait_ge(sem.left, left)
        return
    fc, near, od, _ = peers(T, topo, core)
    V, A, P, Y = g.vector, g.scalar, g.tensor, g.sync

    half = 2 * TC
    for i in range(2):
        Y.dma_start(T.xt[:, half * i:half * i + half], T.x[:, half * i:half * i + half]).then_inc(sem["ldx%d" % i], 16)
    for grp in range(8):
        (Y if grp < 3 else A).dma_start(T.snl[16 * grp:16 * grp + 16, :], T.sn[:]).then_inc(sem.ldsn, 16)
    A.dma_start(T.wt[:], T.w[:]).then_inc(sem.ldw, 16)
    A.dma_start(T.qll[:], T.ql[:]).then_inc(sem.ldql, 16)

    for i in range(2):
        V.wait_ge(sem["ldx%d" % i], 16)
        a, b = TC // 2 * i, TC // 2 * i + TC // 2
        V.quantize_mx(T.xq[:, a:b], T.xs[:, a:b], T.xt[:, 4 * a:4 * b]).then_inc(sem.qx, 1)
    V.wait_ge(sem.ldsn, 128)
    V.tensor_copy(T.offs[:], T.snl[:]).then_inc(sem.coff, 1)
    k = CAPP // 16
    for Q in (V, A):
        Q.wait_ge(sem.qx, 2)
        Q.wait_ge(sem.coff, 1)
    picks = [[near[0]], fc[0], fc[1], [near[1]], [od]]
    for i in (0, 1, 2, 3, 4):
        a, b = picks[i][0], picks[i][-1] + 1
        V.tensor_copy(T.snd[:, CAPP * a:CAPP * b].bitcast(U32),
                      T.xq[:, 0:TC].bitcast(U32).indirect(T.offs[:, k * a:k * b])).then_inc(sem["pc%d" % i], 1)
    for i in (0, 3, 1, 2, 4):
        a, b = picks[i][0], picks[i][-1] + 1
        A.activation(T.snds[:, CAPP * a:CAPP * b],
                     T.xs[:, 0:TC].indirect(T.offs[:, k * a:k * b]), COPY).then_inc(sem["pz%d" % i], 1)

    left = 0
    for need, wave in plan(T, topo, core):
        for s, i in need:
            g.wait_ge(sem["%s%d" % (s, i)], 1)
        left += call(g, T, topo, wave)

    V.quantize_mx(T.have[:, 0:TC], T.haves[:, 0:TC], T.xt[:]).then_inc(sem.qh, 1)
    V.wait_ge(sem.ldql, 16)
    V.tensor_copy(T.offq[:], T.qll[:]).then_inc(sem.coq, 1)
    V.wait_ge(sem.ldw, 16)
    V.quantize_mx(T.wq[:, 0:O * 128], T.ws[:, 0:O * 128], T.wt[:]).then_inc(sem.qw, 1)

    senders = [c for c in cs if c != core]
    senders += [peers(T, topo, c)[3] for c in senders]
    for Q, s in ((V, "arrc"), (A, "arrz")):
        Q.wait_ge(sem.qh, 1)
        Q.wait_ge(sem.coq, 1)
        Q.wait_ge(sem[s], due(T, topo, core, senders, s))
    for h, (a, n) in enumerate(CHUNKS):
        off = T.offq[:, a // 16:(a + n) // 16]
        V.tensor_copy(T.vq[:, a:a + n].bitcast(U32), T.have[:, 0:HV].bitcast(U32).indirect(off)).then_inc(sem["vc%d" % h], 1)
        A.activation(T.vs[:, a:a + n], T.haves[:, 0:HV].indirect(off), COPY).then_inc(sem["vz%d" % h], 1)

    P.wait_ge(sem.qw, 1)
    for h, (b, n) in enumerate(CHUNKS):
        P.wait_ge(sem["vc%d" % h], 1)
        P.wait_ge(sem["vz%d" % h], 1)
        for o in range(O):
            i = 2 * h + o
            acc = T.acc[:, 512 * i:512 * i + n]
            P.matmul_mx(acc, T.wq[:, 128 * o:128 * o + 128], T.ws[:, 128 * o:128 * o + 128],
                        T.vq[:, b:b + n], T.vs[:, b:b + n], True, True).then_inc(sem["mm%d" % i], 1)
            a = S * o + b
            if (h, o) in BY_SCALAR:
                A.wait_ge(sem["mm%d" % i], 1)
                A.activation(T.ysb[:, a:a + n], acc, COPY).then_inc(sem["cp%d" % i], 1)
            else:
                V.wait_ge(sem["mm%d" % i], 1)
                V.tensor_copy(T.ysb[:, a:a + n], acc).then_inc(sem["cp%d" % i], 1)
            Y.wait_ge(sem["cp%d" % i], 1)
            Y.dma_start(T.y[:, a:a + n], T.ysb[:, a:a + n]).then_inc(sem.stored, 16)
    Y.wait_ge(sem.stored, 6 * 16)
    g.wait_ge(sem.left, left)
